import numpy as np, ml_dtypes
CORES = [35,38,43,46]
N = 4
BF = ml_dtypes.bfloat16
V, HB, KB, S, SB, M, CL, RO = 4096, 11, 2048, 192, 64, 1, 24, 3
def hashes(v, a, t):
    u = np.matmul(a.transpose(0, 1, 3, 2), v)
    return np.add.reduce((u > t[..., None]) * (2 ** np.arange(HB))[:, None], axis=2)
def parts(rng):
    a = rng.integers(-8, 9, (1, 8, 16, HB))
    t = np.rint(127.5 * np.add.reduce(a, axis=2) + 700 * rng.standard_normal((1, 8, HB))).astype(np.int64)
    x = rng.integers(0, 256, (N, 8, 16, V)); s = rng.integers(0, 256, (N, 8, 16, S)); b = rng.integers(0, V, (N, 8, 16, KB))
    return x, s, b, a, t
def near(rng, x, s, b, a, t, d, share, twins):
    m = rng.integers(0, V, (N, 8, S)); p = np.take_along_axis(x, m[:, :, None, :], 3)
    v = np.where(rng.random((N, 8, 1, S)) < share, np.clip(p + d, 0, 255), s)
    for q in range(N):
        for g in range(8):
            o = rng.permutation(S); v[q, g][:, o[:twins]] = v[q, g][:, o[twins:2 * twins]]; m[q, g, o[:twins]] = m[q, g, o[twins:2 * twins]]
    b[np.arange(N)[:, None, None], np.arange(8)[None, :, None], rng.integers(0, 16, (N, 8, S)), hashes(v, a, t)] = m
    return v
def pack(x, s, b, a, t):
    w = np.zeros((N, 8, 16, 16), np.float32); w[..., :HB] = a
    z = np.zeros((N, 8, 16), np.int32); z[..., :HB] = t
    return {"nx": x.reshape(N, 128, V).astype(np.float32).astype(BF), "bk": np.ascontiguousarray(b.reshape(N, 128, KB)).astype(np.int32),
            "s0": s.reshape(N, 128, S).astype(np.float32).astype(BF), "pa": w.reshape(N, 128, 16).astype(BF), "th": z.reshape(N, 128, 1)}
def setup_inputs(rng):
    x, s, b, a, t = parts(rng)
    s = near(rng, x, s, b, a, t, rng.integers(-40, 41, s.shape), 0.5, S // 8)
    return pack(x, s, b, a, t)
def setup_inputs_ties(rng):
    x, s, b, a, t = parts(rng)
    pat = rng.integers(0, 256, (N, 8, 16, 24)); x = np.take_along_axis(pat, rng.integers(0, 24, (N, 8, 1, V)), 3)
    s = np.where(rng.random((N, 8, 1, S)) < 0.5, np.take_along_axis(pat, rng.integers(0, 24, (N, 8, 1, S)), 3), s)
    for i in range(HB): t[0, :, i] = np.add.reduce(a[0, :, :, i] * s[i % N, :, :, (7 * i) % S], axis=1)
    return pack(x, s, b, a, t)
def setup_inputs_alike(rng):
    x, s, b, a, t = parts(rng)
    s[:, 0] = s[:, 0, :, :1].copy(); s[:, 1] = np.repeat(s[:, 1, :, :S // 16], 16, axis=2)
    b[:, 2] = rng.choice(np.array([0, 1, V - 2, V - 1]), (N, 16, KB)); t[:, 3] = 32767; t[:, 4] = -32768
    b[:, 5] = b[:, 5, :1].copy(); b[:, 6, :, 1::2] = b[:, 6, :, 0::2]
    t[:, 7] = 32767
    for q in range(N):
        m = 16 * rng.integers(0, V // 16, 2); lo, hi = int(m[0]), int(m[1]) + 8
        x[q, 7][:, lo] = rng.integers(0, 4, 16); x[q, 7][:, hi] = rng.integers(252, 256, 16)
        b[q, 7, :, :M] = hi; b[q, 7, 0, :M] = lo
    s[:, 7] = rng.integers(0, 4, (N, 16, S)); s[:, 7, :, :2] = 255 - s[:, 7, :, :2]
    return pack(x, s, b, a, t)
def setup_inputs_ends(rng):
    x, s, b, a, t = parts(rng)
    x = rng.integers(CL + 1, 255 - CL, x.shape); d = rng.choice(np.array([-CL - 1, -CL, 1 - CL, -1, 0, 1, CL - 1, CL, CL + 1]), s.shape)
    s = near(rng, x, s, b, a, t, d, 0.9, 2)
    x[:, 5] = 255 * rng.integers(0, 2, (N, 16, V)); s[:, 5] = 255 * rng.integers(0, 2, (N, 16, S)); x[:, 6] = 255; s[:, 6] = 0
    e = HB - 1; a[0, 3] = np.eye(16, HB, dtype=np.int64)
    t[0, 3] = CL // 2; t[0, 3, 1::2] = 0; t[0, 3, e] = 2 * CL + CL // 2
    pat = rng.permutation(2 ** e)[:S] + 2 ** e
    on = np.ones((16, S), bool); on[:HB] = ((pat[None, :] >> np.arange(HB)[:, None]) & 1) == 1
    s[:, 3] = np.where(on, rng.integers(128, 161, (N, 16, S)), 0); x[:, 3] = 0
    for q in range(N): b[q, 3, 0, pat] = rng.permutation(V)[:S]
    a[0, 4] = np.where(np.arange(HB) % 2 == 1, -1, 1) * (8 - (rng.random((16, HB)) < 0.125).astype(np.int64))
    a[0, 4, :, 0] = 8; a[0, 4, :, 1] = -8
    t[0, 4] = np.clip(240 * np.add.reduce(a[0, 4], axis=0) + np.rint(250 * rng.standard_normal(HB)).astype(np.int64), -32768, 32767)
    t[0, 4, 0] = 32639; t[0, 4, 1] = -32640
    x[:, 4] = rng.integers(225, 256, (N, 16, V)); s[:, 4] = rng.integers(225, 256, (N, 16, S)); s[:, 4, :, ::8] = 255
    x[:, 7] = rng.integers(253, 256, (N, 16, V)); s[:, 7] = rng.integers(0, 41, (N, 16, S))
    t[0, 7] = np.rint(20 * np.add.reduce(a[0, 7], axis=0) + 100 * rng.standard_normal(HB)).astype(np.int64)
    return pack(x, s, b, a, t)
def setup_inputs_few(rng):
    x, s, b, a, t = parts(rng)
    t[:, :, 5:] = np.where(rng.random((1, 8, HB - 5)) < 0.5, 32767, -32768)
    a[:, 1, :, 6] = 0; t[:, 1, 6] = -1; a[:, 2, :, 7] = 0; t[:, 2, 7] = 0
    s = near(rng, x, s, b, a, t, rng.integers(-60, 61, s.shape), 0.7, S // 8)
    return pack(x, s, b, a, t)
def setup_inputs_spread(rng):
    x, s, b, a, t = parts(rng)
    a = np.where(rng.random(a.shape) < 0.5, 0, a)
    t = np.rint(40 * np.add.reduce(a, axis=2) + 400 * rng.standard_normal((1, 8, HB))).astype(np.int64)
    x = np.minimum((np.exp2(8 * rng.random((N, 8, 1, V))) * rng.random(x.shape)).astype(np.int64), 255)
    s = np.minimum((np.exp2(8 * rng.random((N, 8, 1, S))) * rng.random(s.shape)).astype(np.int64), 255)
    b = np.minimum((V * rng.random(b.shape) ** 3).astype(np.int64), V - 1)
    return pack(x, s, b, a, t)
def check_inputs(d):
    bad = []
    for k, lo, hi in (("nx", 0, 255), ("bk", 0, V - 1), ("s0", 0, 255), ("pa", -8, 8), ("th", -32768, 32767)):
        v = np.asarray(d[k]).astype(np.float64)
        if not np.all((v >= lo) & (v <= hi) & (v == np.floor(v))): bad.append("range of " + k)
    p = np.asarray(d["pa"]).astype(np.float64); z = np.asarray(d["th"]).astype(np.float64)
    if np.any(p != p[:1]): bad.append("pa alike on all ranks")
    if np.any(z != z[:1]): bad.append("th alike on all ranks")
    if np.any(p[:, :, HB:] != 0): bad.append("zeros of pa")
    if np.any(z.reshape(-1, 8, 16)[:, :, HB:] != 0): bad.append("zeros of th")
    return bad
def reference(nx, bk, s0, pa, th):
    x = nx.astype(np.float32).astype(np.int64).reshape(N, 8, 16, V); b = bk.astype(np.int64).reshape(N, 8, 16, KB)
    s = s0.astype(np.float32).astype(np.int64).reshape(N, 8, 16, S)
    a = pa.astype(np.float32).astype(np.int64).reshape(N, 8, 16, 16)[..., :HB]; t = th.astype(np.int64).reshape(N, 8, 16)[..., :HB]
    lower = np.tri(S, S, -1) > 0
    src = (np.arange(N)[:, None] - 1 - np.arange(S)[None, :] // SB) % N
    for rnd in range(RO):
        h = hashes(s, a, t)
        cols = h[..., None] ^ np.arange(M)
        cand = np.take_along_axis(b, cols.reshape(N, 8, 1, S * M), 3).reshape(N, 8, 16, S, M)
        cand = np.ascontiguousarray(cand.transpose(0, 1, 3, 4, 2)).reshape(N, 8, S, 16 * M)
        w = np.take_along_axis(x, cand.reshape(N, 8, 1, S * 16 * M), 3).reshape(N, 8, 16, S, 16 * M)
        dist = np.add.reduce(np.abs(w - s[..., None]), axis=2)
        c = np.take_along_axis(cand, np.argmin(dist, axis=3)[..., None], 3)[..., 0]
        xc = np.take_along_axis(x, c[:, :, None, :], 3)
        x1 = xc + np.clip(s - xc, -CL, CL); h1 = hashes(x1, a, t)
        same = (c[..., :, None] == c[..., None, :]) | (h1[..., :, None] == h1[..., None, :])
        stand = ~np.any(same & lower, axis=3)
        s1 = (s + xc) & 255
        for r in range(N):
            for g in range(8):
                k = np.flatnonzero(stand[r, g]); ck = c[r, g, k]
                x[r, g][:, ck] = x1[r, g][:, k]
                b[r, g, (ck + k) & 15, h1[r, g, k]] = ck
        s = np.take_along_axis(s1, src[:, None, None, :], 0)
    return {"ys": s.reshape(N, 128, S).astype(np.float32), "yb": b.reshape(N, 128, KB).astype(np.float32)}

from concourse.bass import DstId, RemoteDMATransfer
from concourse.mybir import AluOpType, AxisListType, ActivationFunctionType

V, KB, S, SB, RO, CL = 4096, 2048, 192, 64, 3, 24
N0 = 56
B1 = 128
IG = 2
BIG = 8192.0
MAGIC = 12582912.0
PAD = 320


def _sb(cols, dtype, *names):
    return {n: ("sbuf", [128, cols], dtype) for n in names}


SCRATCH = {}
SCRATCH.update(_sb(V + PAD, "bfloat16", "nxw"))
SCRATCH.update(_sb(KB, "int32", "bki"))
SCRATCH.update(_sb(3 * KB + PAD, "float32", "bkw"))
SCRATCH.update(_sb(16 * S, "bfloat16", "xg", "mx"))
SCRATCH.update(_sb(1248, "bfloat16", "ec", "eh"))
SCRATCH.update(_sb(S, "bfloat16", "st0", "st1", "st2", "pay0", "pay1", "dm", "mc", "mv", "rs", "tv",
                   "sg", "dd", "cp", "sy", "sq", "rb", "ae", "xp"))
SCRATCH.update(_sb(S, "float32", "st3", "pay2", "tq", "iot", "candf", "sc", "sh", "sv", "rr", "cb", "on"))
SCRATCH.update(_sb(S, "uint16", "cand"))
SCRATCH.update(_sb(S, "float16", "zz", "cu", "hu"))
SCRATCH.update(_sb(128, "float16", "blkh"))
SCRATCH.update(_sb(128, "bfloat16", "ioi", "ident", "id2", "idn", "idn128", "idn16", "blk", "blkb", "pab", "pan",
                   "wrep", "rk", "f1", "f2"))
SCRATCH.update(_sb(128, "float32", "iog", "pm1", "pm2", "pn1", "pn2"))
SCRATCH.update(_sb(144, "float32", "io128"))
SCRATCH.update(_sb(144, "bfloat16", "wbig"))
SCRATCH.update(_sb(16, "bfloat16", "pas"))
SCRATCH.update(_sb(16, "float32", "col", "two", "zer", "pw", "oh"))
SCRATCH.update(_sb(8, "bfloat16", "gx", "gm"))
SCRATCH.update(_sb(8, "float32", "iog2", "gs"))
SCRATCH.update(_sb(4, "int32", "thi", "pint"))
SCRATCH.update(_sb(12, "float32", "dmy", "lh", "lc"))
SCRATCH.update(_sb(12, "uint16", "hl", "cl", "hp", "lhu", "lcu"))
SCRATCH.update({"p%d" % j: ("psum", [128, 512], "float32") for j in range(8)})
SEMAPHORES = ["cv", "ca", "ct", "cg", "l_s", "l_pa", "l_th", "l_bk", "l_nx", "o_ys", "o_yb",
              "arr0", "arr1", "arr2", "snt"]

A = AluOpType
F = ActivationFunctionType


def engine_split(topo, src, dsts):
    far = [d for d in dsts if topo.chip(d) != topo.chip(src)]
    near = [d for d in dsts if topo.chip(d) == topo.chip(src)]
    used, res = [], {}
    for grp in (far, near):
        if not grp:
            continue
        free = [e for e in topo.engines(src, grp[0]) if e not in used]
        n = 1
        while 2 * n * len(grp) <= len(free):
            n *= 2
        for j, d in enumerate(grp):
            res[d] = free[j * n:(j + 1) * n]
            used += res[d]
    return res


def is_bank(k):
    return k[0] == "p" and k[1:].isdigit()


def emit(ops, queues, csem, T):
    last_w, readers, known, clock = {}, {}, {q: {} for q in queues}, []
    waits, marked = [], set()
    for n, (q, fn, rd, wr, dma) in enumerate(ops):
        need = []
        for k in rd:
            if k in last_w:
                need.append((last_w[k], False))
        for k in wr:
            if k in last_w:
                need.append((last_w[k], is_bank(k)))
            need += [(m, False) for m in readers.get(k, [])]
        best = {}
        for m, bank in need:
            mq, mdma = ops[m][0], ops[m][4]
            if mdma is None and mq == q and (q == "t" or bank):
                continue
            key = mq if mdma is None else ("d", m)
            if known[q].get(key, -1) >= m:
                continue
            best[key] = max(best.get(key, -1), m)
        mine = []
        for key, m in sorted(best.items(), key=lambda kv: -kv[1]):
            if known[q].get(key, -1) >= m:
                continue
            mine.append(m)
            marked.add(m)
            for k2, v2 in clock[m].items():
                if known[q].get(k2, -1) < v2:
                    known[q][k2] = v2
        waits.append(mine)
        ck = dict(known[q])
        ck[q if dma is None else ("d", n)] = n
        clock.append(ck)
        for k in rd:
            readers.setdefault(k, []).append(n)
        for k in wr:
            last_w[k] = n
            readers[k] = []
    count, val = {q: 0 for q in queues}, {}
    for n, (q, fn, rd, wr, dma) in enumerate(ops):
        if dma is not None:
            val[n] = dma
        elif n in marked:
            count[q] += 1
            val[n] = (csem[q], count[q])
    for n, (q, fn, rd, wr, dma) in enumerate(ops):
        for m in waits[n]:
            queues[q].wait_ge(T.sem[val[m][0]], val[m][1])
        ins = fn()
        if ins is not None:
            if dma is not None:
                ins.then_inc(T.sem[dma[0]], 16)
            elif n in marked:
                ins.then_inc(T.sem[csem[q]], 1)


def rank_program(g, core, T, topo):
    rank = T.rank_of(core)
    if rank is None:
        return
    cores = list(T.cores)
    n_ranks = len(cores)
    ops = []
    vec, act, pe = g.vector, g.scalar, g.tensor

    def op(q, fn, rd, wr, dma=None):
        banks = [k for k in rd if is_bank(k)]
        ops.append((q, fn, [k for k in rd if k not in banks], list(wr) + banks, dma))

    def ts(out, in0, s1, s2, o0, o1, rd, wr):
        if o1 is None:
            op("v", lambda: vec.tensor_scalar(out, in0, s1, None, o0), rd, wr)
        else:
            op("v", lambda: vec.tensor_scalar(out, in0, s1, s2, o0, o1), rd, wr)

    def tt(out, in0, in1, o, rd, wr):
        op("v", lambda: vec.tensor_tensor(out, in0, in1, o), rd, wr)

    def cpy(out, in_, rd, wr):
        op("v", lambda: vec.tensor_copy(out, in_), rd, wr)

    def fill(out, c, wr):
        op("v", lambda: vec.memset(out, c), [], wr)

    def scan(out, d0, d1, o0, o1, rd, wr, init=0.0):
        op("v", lambda: vec.tensor_tensor_scan(out, d0, d1, init, o0, o1), rd, wr)

    def av(out, in_, fn, rd, wr, bias=0.0, scale=1.0):
        op("a", lambda: act.activation(out, in_, fn, bias=bias, scale=scale), rd, wr)

    def mm(out, lhs, rhs, st, sp, rd, wr):
        op("t", lambda: pe.matmul(out, lhs, rhs, st, sp), rd, wr)

    def iota(out, pat, base, cm, wr, flag=True):
        if flag:
            op("g", lambda: g.iota(out, pat, base, cm, allow_small_or_imprecise_dtypes=True), [], wr)
        else:
            op("g", lambda: g.iota(out, pat, base, cm), [], wr)

    op("s", lambda: g.sync.dma_start(T.st0[:], T.s0[:]), [], ["st0"], ("l_s", 16))
    op("s", lambda: g.sync.dma_start(T.bki[:], T.bk[:]), [], ["bki"], ("l_bk", 16))
    op("s", lambda: g.sync.dma_start(T.nxw[:, 0:V], T.nx[:]), [], ["nxw"], ("l_nx", 16))
    op("a", lambda: act.dma_start(T.pas[:], T.pa[:]), [], ["pas"], ("l_pa", 16))
    op("a", lambda: act.dma_start(T.thi[:, 0:1], T.th[:]), [], ["thi"], ("l_th", 16))

    c = T.col
    gf, pf, pp, w1, thf, thb, c15 = (c[:, j:j + 1] for j in range(7))
    iota(T.pint[:, 0:1], [[0, 1]], 0, 1, ["pint"], False)
    iota(T.iog2[:], [[1, 8]], 0, 0, ["iog2"])
    iota(T.iog[:], [[1, 8], [0, 16]], 0, 0, ["iog"])
    iota(T.io128[:], [[1, 144]], 0, 0, ["io128"])
    iota(T.tq[:], [[0, 12], [1, 16]], 0, 0, ["tq"])
    iota(T.iot[:], [[1, S]], 0, 0, ["iot"])
    iota(T.ioi[:], [[0, 8], [1, 16]], 0, 0, ["ioi"])
    iota(T.dmy[:], [[16, 12]], 2048, 1, ["dmy"])
    fill(T.two[:], 2.0, ["two"])
    fill(T.zer[:], 0.0, ["zer"])
    scan(T.pw[:, 0:11], T.two[:, 0:11], T.zer[:, 0:11], A.mult, A.add, ["two", "zer"], ["pw0"], 0.25)
    fill(T.pw[:, 11:12], -1024.0, ["pw1"])
    fill(T.pw[:, 12:13], 0.5, ["pw2"])
    fill(T.pw[:, 13:16], 0.0, ["pw3"])
    ts(T.pint[:, 1:2], T.pint[:, 0:1], 4, None, A.arith_shift_right, None, ["pint"], ["pint1"])
    ts(T.pint[:, 2:3], T.pint[:, 0:1], 15, None, A.bitwise_and, None, ["pint"], ["pint2"])
    cpy(pp, T.pint[:, 0:1], ["pint"], ["pp"])
    cpy(gf, T.pint[:, 1:2], ["pint1"], ["gf"])
    cpy(pf, T.pint[:, 2:3], ["pint2"], ["pf"])
    ts(T.gs[:], T.iog2[:], gf, None, A.is_equal, None, ["iog2", "gf"], ["gs"])
    ts(T.blk[:], T.iog[:], gf, None, A.is_equal, None, ["iog", "gf"], ["blk"])
    ts(T.oh[:], T.io128[:, 0:16], pf, None, A.is_equal, None, ["io128", "pf"], ["oh"])
    ts(c15, gf, 16.0, 15.0, A.mult, A.add, ["gf"], ["c15"])
    ts(T.ident[:], T.io128[:, 0:128], pp, None, A.is_equal, None, ["io128", "pp"], ["ident"])
    tt(T.oh[:], T.oh[:], T.pw[:], A.mult, ["oh", "pw0", "pw1", "pw2", "pw3"], ["oh"])
    cpy(T.blkh[:], T.blk[:], ["blk"], ["blkh"])
    op("v", lambda: vec.tensor_reduce(w1, T.oh[:], AxisListType.X, A.add), ["oh"], ["w1"])
    ts(T.dm[:], T.tq[:], pf, None, A.is_equal, None, ["tq", "pf"], ["dm"])
    ts(T.wbig[:], T.io128[:], c15, w1, A.is_equal, A.mult, ["io128", "c15", "w1"], ["wbig"])
    ts(T.rs[:], T.tq[:], 0.0, -2.0 ** 24, A.is_equal, A.mult, ["tq"], ["rs"])
    ts(T.rk[:], T.tq[:, 0:128], 0.0, 2.0 ** 20, A.is_equal, A.mult, ["tq"], ["rk"])
    ts(T.mv[:], T.dm[:], 2.0 ** 23 - 2 * BIG - 4096.0, -2.0 ** 23, A.mult, A.add, ["dm"], ["mv"])
    ts(T.tv[:], T.iot[:], pf, None, A.subtract, None, ["iot", "pf"], ["tv"])
    cpy(thf, T.thi[:, 0:1], ["thi"], ["thf"])
    ts(thb, thf, -1.0, -0.5, A.mult, A.add, ["thf"], ["thb"])
    for j in range(8):
        av(T.pab[:, 16 * j:16 * j + 16], T.pas[:], F.Copy, ["pas", "gs"], ["pab%d" % j], scale=T.gs[:, j:j + 1])
    pabk = ["pab%d" % j for j in range(8)]
    av(T.wrep[:], T.blk[:], F.Copy, ["blk", "w1"], ["wrep"], scale=w1)
    av(T.mc[:], T.dm[:], F.Identity, ["dm"], ["mc"], scale=BIG, bias=-BIG)
    av(T.gx[:], T.gs[:], F.Copy, ["gs"], ["gx"], scale=-16.0)
    av(T.gm[:], T.gs[:], F.Copy, ["gs"], ["gm"], scale=32.0)
    av(T.pan[:], T.pab[:], F.Copy, pabk, ["pan"], scale=-1.0)
    av(T.blkb[:], T.blk[:], F.Copy, ["blk"], ["blkb"], scale=BIG)
    for nm, val in (("id2", 2.0), ("idn", -1.0), ("idn128", -128.0), ("idn16", -16.0)):
        av(T[nm][:], T.ident[:], F.Copy, ["ident"], [nm], scale=val)

    dsts = [cores[(rank + 1 + j) % n_ranks] for j in range(S // SB)]
    split = engine_split(topo, core, dsts)
    arrive = 0
    for q in range(n_ranks):
        if q != rank:
            arrive += len(engine_split(topo, cores[q], [cores[(q + 1 + j) % n_ranks] for j in range(S // SB)])[core])
    sent = sum(len(e) for e in split.values())
    near = [j for j, d in enumerate(dsts) if topo.chip(d) == topo.chip(core)]
    jb = 0 if near == [0] else len(dsts) - 1
    b0, a0 = SB * jb, (SB if jb == 0 else 0)
    b1, a1 = b0 + SB, a0 + B1

    def send(r, part):
        trs = []
        for j in part:
            rid, pid, _se = topo.addr(dsts[j])
            trs.append(RemoteDMATransfer(
                dst_ids=[DstId(rid=rid, pnc=pid)], dma_engine_mask=sum(1 << e for e in split[dsts[j]]),
                remote_sem=T.sem["arr%d" % r], src=T["pay%d" % r][:, SB * j:SB * j + SB],
                dst=T["st%d" % (r + 1)][:, SB * j:SB * j + SB]))
        g.remote_dma_fused(trs, local_sem=T.sem.snt)

    ps, pu, phw, pcr = T.p0[:, 0:S], T.p1[:, 0:S], T.p1[:, 256:268], T.p1[:, 320:512]
    pcm, pvv, pqb = T.p2[:, 0:S], T.p2[:, 0:S], T.p3[:, 0:S]
    phm, pe_, py, pq = T.p4[:, 0:S], T.p5[:, 0:S], T.p6[:, 0:S], T.p7[:, 0:S]
    win = T.nxw[:, 0:V]
    m2 = S - B1

    def runs(name):
        res, at = [], S
        for k in range(11):
            n = S - 16 * (k + 1)
            res.append((k, at, n, "e%s%d" % (name, k)))
            at += n
        return res

    def pairs(name, rep, own, ownk, ebuf):
        for k, at, n, kk in runs(name):
            ts(ebuf[:, at:at + n], rep[:, S - n:S], own[:, 16 * k + 15:16 * k + 16], None, A.is_equal, None,
               [name + "u1", name + "u2"] + ownk, [kk])

    def count(name, ebuf, a, b, stop):
        for k, at, n, kk in runs(name)[a:b]:
            mm(pvv[:, S - n:S], T.blkb[:], ebuf[:, at:at + n], False, stop and k == b - 1, ["blkb", kk], ["p2"])

    def hash_states(r):
        s, sk = T["st%d" % r], "st%d" % r
        if r:
            op("t", lambda: None, [], [sk], ("arr%d" % (r - 1), arrive))
        mm(pu, T.pab[:], s[:], True, True, pabk + [sk], ["p1"])
        mm(ps, T.ident[:], s[:], True, True, ["ident", sk], ["p0"])
        av(T.sg[:], pu, F.Sign, ["p1", "thb"], ["sg"], bias=thb)
        for j in range(16):
            mm(phw, T.wbig[:, 15 - j:143 - j], T.sg[:, j::16], j == 0, j == 15, ["wbig", "sg"], ["p1"])
        cpy(T.hl[:], phw, ["p1"], ["hl"])

    hash_states(0)
    cpy(T.cand[:], T.bki[:].indirect(T.hl[:]), ["bki", "hl"], ["cand"])
    cpy(T.bkw[:, 0:KB], T.bki[:], ["bki"], ["bkw"])
    ts(T.candf[:], T.cand[:], -2048.0, None, A.add, None, ["cand"], ["candf"])
    for r in range(RO):
        s, sk, last = T["st%d" % r], "st%d" % r, r == RO - 1
        am = a0 + SB
        av(T.xg[:, 16 * (a0 + N0):16 * am], win.indirect(T.cand[:, a0 + N0:am]), F.Copy, ["nxw", "cand"], ["xg0a"])
        av(T.xg[:, 16 * am:16 * a1], win.indirect(T.cand[:, am:a1]), F.Copy, ["nxw", "cand"], ["xg1"])
        av(T.xg[:, 16 * b0:16 * b1], win.indirect(T.cand[:, b0:b1]), F.Copy, ["nxw", "cand"], ["xg2"])
        cpy(T.xg[:, 16 * a0:16 * (a0 + N0)], win.indirect(T.cand[:, a0:a0 + N0]), ["nxw", "cand"], ["xg0"])

        def larger(t0, t1, i, xk, name):
            tt(T.mx[:, 16 * t0 + i:16 * t1:16], T.xg[:, 16 * t0 + i:16 * t1:16], ps[:, t0:t1], A.max,
               xk + ["p0"], [name])

        def head(b, t0, t1, xk):
            kb, bank, m = (T.p2, T.p3)[b], "p%d" % (2 + b), t1 - t0
            mm(kb[0:m, 0:128], T.ident[:, 0:m], T.ioi[:], True, False, ["ident", "ioi"], [bank])
            for i in range(16 if b == 0 else 0):
                mm(kb[0:m, i:128:16], T.xg[:, 16 * t0 + i:16 * t1:16], T.gx[:], False, False, xk + ["gx"], [bank])

        def body(b, t0, t1, xk, lo, more, ia, ib):
            kb, bank, m = (T.p2, T.p3)[b], "p%d" % (2 + b), t1 - t0
            for i0 in range(ia, ib, IG):
                for i in range(i0, i0 + IG):
                    larger(lo, t1, i, xk, "mx%d_%d" % (b, i))
                for i in range(i0, i0 + IG if b else i0):
                    mm(kb[0:m, i:128:16], T.xg[:, 16 * t0 + i:16 * t1:16], T.gx[:], False, False, xk + ["gx"], [bank])
                for i in range(i0, i0 + IG):
                    mm(kb[0:m, i:128:16], T.mx[:, 16 * t0 + i:16 * t1:16], T.gm[:], False, i == 15,
                       ["mx%d_%d" % (b, i0 + IG - 1), "mx%d_%d" % (b, i), "gm"] + more, [bank])

        def bb(ia, ib):
            body(1, b0, b1, ["xg2"], b0, [], ia, ib)

        for i in range(16):
            larger(a0, am, i, ["xg0", "xg0a"], "mxa%d" % i)
        head(0, a0, a1, ["xg0", "xg0a", "xg1"])
        body(0, a0, a1, ["xg1"], am, ["mxa%d" % i for i in range(16)], 0, 16)
        ca, cb_, ka, kb_ = slice(a0, a1), slice(b0, b1), slice(a0 // 16, a1 // 16), slice(b0 // 16, b1 // 16)
        pay, pk = T["pay%d" % r], "pay%d" % r
        head(1, b0, b1, ["xg2"])
        bb(0, 2)
        scan(T.pm1[:], T.rk[:], T.p2[:, 0:128], A.max, A.min, ["rk", "p2"], ["pm1"])
        bb(2, 4)
        scan(T.pn1[:, ::-1], T.rk[:], T.pm1[:, ::-1], A.max, A.min, ["rk", "pm1"], ["pn1"])
        bb(4, 6)
        tt(T.f1[:], T.pn1[:], T.p2[:, 0:128], A.is_equal, ["pn1", "p2"], ["f1"])
        mm(T.p4[:, 0:B1], T.f1[:], T.ident[:], True, True, ["f1", "ident"], ["p4"])
        mm(pcm[:, ca], T.ident[:], T.mc[:, ca], True, False, ["ident", "mc"], ["p2"])
        bb(6, 10)
        tt(T.zz[:, ca], T.candf[:, ca], T.p4[:, 0:B1], A.mult, ["candf", "p4"], ["zz1"])
        mm(pcm[:, ca], T.blkh[:], T.zz[:, ca], False, True, ["blkh", "zz1"], ["p2"])
        bb(10, 14)
        scan(T.sc[:, ca], T.rs[:, ca], pcm[:, ca], A.add, A.max, ["rs", "p2"], ["sc1"])
        bb(14, 16)
        ts(T.cl[:, ka], T.sc[:, a0 + 15:a1:16], 2048.0, None, A.add, None, ["sc1"], ["cl1"])
        mm(py[:, ca], T.id2[:], s[:, ca], True, False, ["id2", sk], ["p6"])
        mm(pe_[:, ca], T.id2[:], s[:, ca], True, False, ["id2", sk], ["p5"])
        mm(pq[:, ca], T.pab[:], s[:, ca], True, False, pabk + [sk], ["p7"])
        mm(pcr[:, ca], T.blkh[:], T.zz[:, ca], True, True, ["blkh", "zz1"], ["p1"])
        mm(pcm[:, cb_], T.ident[:], T.mc[:, cb_], True, False, ["ident", "mc"], ["p2"])
        tt(T.dd[:, ca], win.indirect(T.cl[:, ka]), s[:, ca], A.subtract, ["nxw", "cl1", sk], ["dd1"])
        mm(py[:, ca], T.ident[:], T.dd[:, ca], False, True, ["ident", "dd1"], ["p6"])
        mm(pq[:, ca], T.pab[:], T.dd[:, ca], False, False, pabk + ["dd1"], ["p7"])
        mm(pe_[:, ca], T.ident[:], T.dd[:, ca], False, False, ["ident", "dd1"], ["p5"])
        av(T.sy[:, ca], py[:, ca], F.Sign, ["p6"], ["sy1"], bias=-255.5)
        scan(T.pm2[0:m2, :], T.rk[0:m2, :], T.p3[0:m2, 0:128], A.max, A.min, ["rk", "p3"], ["pm2"])
        ts(T.cp[:, ca], T.dd[:, ca], -float(CL), float(CL), A.max, A.min, ["dd1"], ["cp1"])
        scan(T.pn2[0:m2, ::-1], T.rk[0:m2, :], T.pm2[0:m2, ::-1], A.max, A.min, ["rk", "pm2"], ["pn2"])
        cpy(T.cu[:, ca], pcr[:, ca], ["p1"], ["cu1"])
        tt(T.f2[0:m2, :], T.pn2[0:m2, :], T.p3[0:m2, 0:128], A.is_equal, ["pn2", "p3"], ["f2"])
        mm(pq[:, ca], T.pan[:], T.cp[:, ca], False, True, ["pan", "cp1"], ["p7"])
        mm(pe_[:, ca], T.idn128[:], T.sy[:, ca], False, True, ["idn128", "sy1"], ["p5"])
        mm(T.p4[:, 0:m2], T.f2[0:m2, :], T.ident[0:m2, 0:m2], True, True, ["f2", "ident"], ["p4"])
        av(pay[:, ca], pe_[:, ca], F.Identity, ["p5"], [pk + "a"], bias=-128.0)
        op("g", lambda r=r: send(r, [j for j in range(len(dsts)) if j != jb]), [pk + "a"], [])
        av(T.sq[:, ca], pq[:, ca], F.Sign, ["p7", "thb"], ["sq1"], bias=thb)
        tt(T.ec[:, ca], T.sc[:, ca], pcr[:, ca], A.is_equal, ["sc1", "p1"], ["ecd1"])
        tt(T.zz[:, cb_], T.candf[:, cb_], T.p4[:, 0:m2], A.mult, ["candf", "p4"], ["zz2"])
        zk = ["blkh", "zz1", "zz2"]
        mm(pcm[:, cb_], T.blkh[:], T.zz[:, cb_], False, True, zk, ["p2"])
        mm(pcr[:, cb_], T.blkh[:], T.zz[:, cb_], True, True, zk, ["p1"])
        mm(phm[:, ca], T.ident[:], T.mc[:, ca], True, False, ["ident", "mc"], ["p4"])
        mm(phm[:, ca], T.wrep[:], T.sq[:, ca], False, True, ["wrep", "sq1"], ["p4"])
        mm(pq[:, ca], T.wrep[:], T.sq[:, ca], True, True, ["wrep", "sq1"], ["p7"])
        mm(py[:, cb_], T.id2[:], s[:, cb_], True, False, ["id2", sk], ["p6"])
        mm(pqb[:, cb_], T.pab[:], s[:, cb_], True, False, pabk + [sk], ["p3"])
        mm(pe_, T.ident[:], T.tv[:], True, False, ["ident", "tv"], ["p5"])
        mm(pe_, T.blkh[:], T.zz[:], False, True, zk, ["p5"])
        scan(T.sc[:, cb_], T.rs[:, cb_], pcm[:, cb_], A.add, A.max, ["rs", "p2"], ["sc2"])
        av(T.rr[:], pe_, F.Identity, ["p5"], ["rr"], bias=MAGIC, scale=0.0625)
        cpy(T.cu[:, cb_], pcr[:, cb_], ["p1"], ["cu2"])
        ts(T.cl[:, kb_], T.sc[:, b0 + 15:b1:16], 2048.0, None, A.add, None, ["sc2"], ["cl2"])
        tt(T.ec[:, cb_], T.sc[:, cb_], pcr[:, cb_], A.is_equal, ["sc2", "p1"], ["ecd2"])
        mm(pvv, T.ident[:], T.mv[:], True, False, ["ident", "mv"], ["p2"])
        mm(pu[:, cb_], T.id2[:], s[:, cb_], True, False, ["id2", sk], ["p1"])
        tt(T.dd[:, cb_], win.indirect(T.cl[:, kb_]), s[:, cb_], A.subtract, ["nxw", "cl2", sk], ["dd2"])
        scan(T.sh[:, ca], T.rs[:, ca], phm[:, ca], A.add, A.max, ["rs", "p4"], ["sh1"])
        ts(T.cp[:, cb_], T.dd[:, cb_], -float(CL), float(CL), A.max, A.min, ["dd2"], ["cp2"])
        cpy(T.hu[:, ca], pq[:, ca], ["p7"], ["hu1"])
        tt(T.eh[:, ca], T.sh[:, ca], pq[:, ca], A.is_equal, ["sh1", "p7"], ["ehd1"])
        pairs("c", T.cu, T.sc, ["sc1", "sc2"], T.ec)
        mm(py[:, cb_], T.ident[:], T.dd[:, cb_], False, True, ["ident", "dd2"], ["p6"])
        mm(pqb[:, cb_], T.pab[:], T.dd[:, cb_], False, False, pabk + ["dd2"], ["p3"])
        mm(pu[:, cb_], T.ident[:], T.dd[:, cb_], False, False, ["ident", "dd2"], ["p1"])
        mm(pqb[:, cb_], T.pan[:], T.cp[:, cb_], False, True, ["pan", "cp2"], ["p3"])
        mm(phm[:, cb_], T.ident[:], T.mc[:, cb_], True, False, ["ident", "mc"], ["p4"])
        mm(pvv, T.blkb[:], T.ec[:, 0:S], False, False, ["blkb", "ecd1", "ecd2"], ["p2"])
        av(T.sy[:, cb_], py[:, cb_], F.Sign, ["p6"], ["sy2"], bias=-255.5)
        av(T.sq[:, cb_], pqb[:, cb_], F.Sign, ["p3", "thb"], ["sq2"], bias=thb)
        mm(pu[:, cb_], T.idn128[:], T.sy[:, cb_], False, True, ["idn128", "sy2"], ["p1"])
        mm(phm[:, cb_], T.wrep[:], T.sq[:, cb_], False, True, ["wrep", "sq2"], ["p4"])
        mm(pq[:, cb_], T.wrep[:], T.sq[:, cb_], True, True, ["wrep", "sq2"], ["p7"])
        av(pay[:, cb_], pu[:, cb_], F.Identity, ["p1"], [pk + "b"], bias=-128.0)
        op("g", lambda r=r: send(r, [jb]), [pk + "b"], [])
        av(T.rb[:], T.rr[:], F.Identity, ["rr"], ["rb"], bias=-MAGIC)
        count("c", T.ec, 0, 4, False)
        mm(pe_, T.ident[:], T.tv[:], True, False, ["ident", "tv"], ["p5"])
        mm(pe_, T.blkh[:], T.zz[:], False, False, zk, ["p5"])
        mm(pe_, T.idn16[:], T.rb[:], False, True, ["idn16", "rb"], ["p5"])
        av(T.ae[:], pe_, F.Abs, ["p5"], ["ae"], scale=4096.0)
        count("c", T.ec, 4, 11, False)
        mm(pvv, T.wrep[:], T.sq[:], False, False, ["wrep", "sq1", "sq2"], ["p2"])
        scan(T.sh[:, cb_], T.rs[:, cb_], phm[:, cb_], A.add, A.max, ["rs", "p4"], ["sh2"])
        cpy(T.hu[:, cb_], pq[:, cb_], ["p7"], ["hu2"])
        tt(T.eh[:, cb_], T.sh[:, cb_], pq[:, cb_], A.is_equal, ["sh2", "p7"], ["ehd2"])
        cpy(T.hp[:], T.sh[:, 15::16], ["sh1", "sh2"], ["hp"])
        pairs("h", T.hu, T.sh, ["sh1", "sh2"], T.eh)
        mm(pvv, T.blkb[:], T.eh[:, 0:S], False, False, ["blkb", "ehd1", "ehd2"], ["p2"])
        count("h", T.eh, 0, 11, True)
        mm(pqb, T.blkh[:], T.zz[:], True, False, zk, ["p3"])
        mm(pqb, T.idn[:], T.ae[:], False, True, ["idn", "ae"], ["p3"])
        av(T.cb[:], pqb, F.Identity, ["p3"], ["cb"], bias=2048.0)
        if not last:
            mm(phm, T.ident[:], s[:], True, False, ["ident", sk], ["p4"])
            mm(phm, T.ident[:], T.dd[:], False, False, ["ident", "dd1", "dd2"], ["p4"])
            mm(phm, T.idn[:], T.cp[:], False, True, ["idn", "cp1", "cp2"], ["p4"])
            av(T.xp[:], phm, F.Copy, ["p4"], ["xp"])
        tt(T.on[:], T.bkw[:, 0:KB].indirect(T.hp[:]), T.ae[:], A.min, ["bkw", "hp", "ae"], ["on"])
        scan(T.sv[:], T.rs[:], pvv, A.add, A.max, ["rs", "p2"], ["sv"])
        tt(T.lh[:], T.sv[:, 15::16], T.dmy[:], A.min, ["sv", "dmy"], ["lh"])
        ts(T.lhu[:], T.lh[:], 4096.0, None, A.add, None, ["lh"], ["lhu"])
        if not last:
            tt(T.lc[:], T.lh[:], T.sc[:, 15::16], A.max, ["lh", "sc1", "sc2"], ["lc"])
        tt(T.bkw[:].indirect(T.lhu[:]), T.on[:], T.cb[:], A.max, ["on", "cb", "lhu"], ["bkw"])
        if not last:
            ts(T.lcu[:], T.lc[:], 2048.0, None, A.add, None, ["lc"], ["lcu"])
            cpy(T.nxw[:].indirect(T.lcu[:]), T.xp[:], ["xp", "lcu"], ["nxw"])
            hash_states(r + 1)
            av(T.candf[:], T.bkw[:, 0:KB].indirect(T.hl[:]), F.Identity, ["bkw", "hl"], ["candf"], bias=-2048.0)
            cpy(T.cand[:], T.bkw[:, 0:KB].indirect(T.hl[:]), ["bkw", "hl"], ["cand"])

    op("s", lambda: g.sync.dma_start(T.yb[:], T.bkw[:, 0:KB]), ["bkw"], ["yb"], ("o_yb", 16))
    op("a", lambda: None, [], ["st3"], ("arr%d" % (RO - 1), arrive))
    op("a", lambda: act.dma_start(T.ys[:], T.st3[:]), ["st3"], ["ys"], ("o_ys", 16))
    op("s", lambda: None, ["yb"], [])
    op("a", lambda: None, ["ys"], [])
    emit(ops, {"v": vec, "a": act, "t": pe, "g": g, "s": g.sync},
         {"v": "cv", "a": "ca", "t": "ct", "g": "cg", "s": "cs"}, T)
    g.wait_ge(T.sem.snt, RO * sent)
